import numpy as np
import ml_dtypes


def mxq(x, axis, fmt="e4m3"):
    dtype, down = {"e4m3": (ml_dtypes.float8_e4m3fn, 7), "e5m2": (ml_dtypes.float8_e5m2, 14)}[fmt]
    v = np.moveaxis(np.asarray(x, np.float32).astype(ml_dtypes.bfloat16).astype(np.float64), axis, -1)
    blocks = v.reshape(v.shape[:-1] + (-1, 32))
    amax = np.abs(blocks).max(-1, keepdims=True)
    byte = np.maximum(np.where(amax > 0, np.frexp(amax)[1] - 1 + 127, 0) - down, 1)
    scale = np.exp2(byte - 127.0)
    codes = (blocks / scale).astype(np.float32).astype(dtype).astype(np.float64)
    return np.moveaxis((codes * scale).reshape(v.shape), -1, axis)


WIDE = False


def mx_kscale(k):
    if not WIDE:
        return np.ones(k)
    levels = np.array([30, -30])
    if k % 512:
        return np.exp2(np.random.permutation(np.resize(levels, k // 32))).repeat(32)
    a = np.empty((k // 512, 16))
    for p in range(k // 512):
        a[p, :8] = np.random.permutation(np.resize(levels, 8))
        for g in range(8):
            far = levels[np.abs(levels - a[p, g]) >= 10]
            a[p, g + 8] = far[np.random.randint(len(far))]
    return np.exp2(a.ravel()).repeat(32)


def f64(x):
    return np.asarray(x).astype(np.float64)


K, L, M, N = 2048, 512, 1024, 512


def setup_inputs():
    n = np.random.standard_normal
    s1 = mx_kscale(K)[:, None]
    s2 = mx_kscale(L)[:, None]
    m1, m2 = np.exp(0.5 * n((1, M))), np.exp(0.5 * n((1, N)))
    return {
        "x": (n((K, M)) / np.sqrt(K) * s1).astype(np.float32),
        "xt": (n((K, N)) / s1).astype(np.float32),
        "g": (m1 * n((L, M)) / np.sqrt(L) * s2).astype(np.float32),
        "gt": (m2 * n((L, N)) / s2).astype(np.float32),
        "r": (n((1024, 512))).astype(np.float32),
    }


def reference(x, xt, g, gt, r):
    x_ = mxq(f64(x), 0, "e4m3")
    xt_ = mxq(f64(xt), 0, "e4m3")
    g_ = mxq(f64(g), 0, "e5m2")
    gt_ = mxq(f64(gt), 0, "e5m2")
    y = x_.T @ xt_
    u = g_.T @ gt_
    y = y * u
    return f64(r) + y

@@ -1,0 +1,173 @@
+from contextlib import ExitStack
+
+import concourse.mybir as mybir
+
+K, L, M, N = 2048, 512, 1024, 512
+FLOPS = 2 * (K + L) * M * N
+
+F32 = mybir.dt.float32
+BF16 = mybir.dt.bfloat16
+U32 = mybir.dt.uint32
+U8 = mybir.dt.uint8
+E4M3 = mybir.dt.float8_e4m3fn_x4
+E5M2 = mybir.dt.float8_e5m2_x4
+MULT = mybir.AluOpType.mult
+ADD = mybir.AluOpType.add
+
+P = 128
+PACK = 4
+K_PASS = P * PACK
+PASSES = K // K_PASS
+TILES = M // P
+
+
+def tile_mix_ghost_res_kernel(tc, x, xt, g, gt, r, out):
+    nc = tc.nc
+    formats = {"x": E4M3, "xt": E4M3, "g": E5M2, "gt": E5M2}
+    sources = {"x": x, "xt": xt, "g": g, "gt": gt}
+
+    with ExitStack() as ctx:
+        keep = ctx.enter_context(tc.tile_pool(name="keep", bufs=1))
+        stage = ctx.enter_context(tc.tile_pool(name="stage", bufs=6))
+        psum = ctx.enter_context(tc.psum_pool(name="psum", bufs=8))
+        ctx.enter_context(tc.manual_schedule())
+
+        raw = {}
+        r_rows = {}
+
+        def load(name, k, c0, c1):
+            tile = keep.tile([P, PACK, c1 - c0], F32, name="raw_%s_%d_%d" % (name, k, c0))
+            rows = sources[name][k * K_PASS : (k + 1) * K_PASS, c0:c1]
+            nc.sync.dma_start(out=tile[:], in_=rows.rearrange("(p j) w -> p j w", j=PACK))
+            raw[name, k] = raw.get((name, k), []) + [(c0, c1, tile)]
+
+        def load_r(t0, t1):
+            tile = keep.tile([P, t1 - t0, N], F32, name="r_%d" % t0)
+            nc.sync.dma_start(out=tile[:], in_=r[t0 * P : t1 * P, :].rearrange("(t p) n -> p t n", p=P))
+            for t in range(t0, t1):
+                r_rows[t] = (t0, tile)
+
+        load("gt", 0, 0, N)
+        load("g", 0, 0, M)
+        for k in (0, 1):
+            load("xt", k, 0, N)
+            load("x", k, 0, M)
+        for k in (2, 3):
+            load("xt", k, 0, N)
+            load("x", k, 0, 512)
+        load("x", 3, 512, 768)
+        load("x", 2, 512, M)
+        load_r(0, 4)
+        load("x", 3, 768, M)
+        load_r(4, 8)
+
+        def interleave(name, k, c0, c1, vector_columns):
+            first, tile = [(a, t) for a, b, t in raw[name, k] if a <= c0 and c1 <= b][0]
+            grouped = stage.tile([P, c1 - c0, PACK], BF16, name="grouped", align_bytes=64)
+            for engine_copy, lo, hi in (
+                (nc.scalar.copy, vector_columns, c1 - c0),
+                (nc.vector.tensor_copy, 0, vector_columns),
+            ):
+                if lo < hi:
+                    engine_copy(
+                        out=grouped[:, lo:hi, :].rearrange("p (c i) j -> p c j i", i=4),
+                        in_=tile[:, :, c0 - first + lo : c0 - first + hi].rearrange("p j (c i) -> p c j i", i=4),
+                    )
+            return grouped
+
+        quantized = {}
+
+        def quantize(name, k, c0, c1, grouped):
+            codes = keep.tile([P, c1 - c0], U32, name="codes_%s_%d_%d" % (name, k, c0), align_bytes=64)
+            scales = keep.tile([P, c1 - c0], U8, name="scales_%s_%d_%d" % (name, k, c0), align_bytes=64)
+            nc.vector.quantize_mx(
+                out=codes[:].bitcast(formats[name]), scales=scales[:], in_=grouped[:].rearrange("p w j -> p (w j)")
+            )
+            quantized[name, k] = quantized.get((name, k), []) + [(c0, c1, codes, scales)]
+
+        def convert(name, k, width):
+            pieces = [(c, c + 512) for c in range(0, width, 512)]
+            grouped = [interleave(name, k, c0, c1, 256) for c0, c1 in pieces]
+            for (c0, c1), tile in zip(pieces, grouped):
+                quantize(name, k, c0, c1, tile)
+
+        def mx_pass(acc, left, right, k, m, start, stop):
+            c0, codes, scales = [(a, co, sc) for a, b, co, sc in quantized[left, k] if a <= m * P < b][0]
+            cols = slice(m * P - c0, (m + 1) * P - c0)
+            right_codes, right_scales = quantized[right, k][0][2:]
+            nc.tensor.matmul_mx(
+                out=acc[:],
+                lhsT=codes[:, cols].bitcast(formats[left]),
+                lhsT_scale=scales[:, cols],
+                rhs=right_codes[:].bitcast(formats[right]),
+                rhs_scale=right_scales[:],
+                start=start,
+                stop=stop,
+            )
+
+        u_acc = {}
+        u = keep.tile([P, TILES, N], F32, name="u")
+        a_acc = {}
+        result = keep.tile([P, TILES, N], F32, name="result")
+
+        def u_passes():
+            for m in range(TILES):
+                u_acc[m] = psum.tile([P, N], F32, name="acc")
+                mx_pass(u_acc[m], "g", "gt", 0, m, True, True)
+
+        def a_passes(k, tiles):
+            for m in tiles:
+                if k == 0:
+                    a_acc[m] = psum.tile([P, N], F32, name="acc")
+                mx_pass(a_acc[m], "x", "xt", k, m, k == 0, k == PASSES - 1)
+
+        def multiply(*tiles):
+            for m in tiles:
+                nc.vector.tensor_tensor(out=result[:, m, :], in0=a_acc[m][:], in1=u[:, m, :], op=MULT)
+
+        def add_and_store(t0, t1):
+            first, tile = r_rows[t0]
+            sums = result[:, t0:t1, :]
+            nc.vector.tensor_tensor(out=sums, in0=sums, in1=tile[:, t0 - first : t1 - first, :], op=ADD)
+            nc.sync.dma_start(out=out[t0 * P : t1 * P, :].rearrange("(t p) n -> p t n", p=P), in_=sums)
+
+        convert("gt", 0, N)
+        convert("g", 0, M)
+        u_passes()
+        convert("xt", 0, N)
+        for m in range(TILES):
+            nc.scalar.copy(out=u[:, m, :], in_=u_acc[m][:])
+        convert("x", 0, M)
+        a_passes(0, range(TILES))
+        convert("xt", 1, N)
+        convert("x", 1, M)
+        a_passes(1, range(TILES))
+        convert("xt", 2, N)
+        convert("x", 2, 512)
+        a_passes(2, range(4))
+        convert("xt", 3, N)
+
+        quantize("x", 3, 0, 512, interleave("x", 3, 0, 512, 320))
+        a_passes(3, range(4))
+        x3_b = interleave("x", 3, 512, 768, 96)
+        multiply(0, 1)
+        quantize("x", 3, 512, 768, x3_b)
+        x2_b = interleave("x", 2, 512, 768, 64)
+        multiply(2, 3)
+        quantize("x", 2, 512, 768, x2_b)
+        a_passes(2, (4, 5))
+        a_passes(3, (4, 5))
+        x2_c = interleave("x", 2, 768, M, 0)
+        x3_c = interleave("x", 3, 768, M, 0)
+        add_and_store(0, 2)
+        multiply(4)
+        quantize("x", 2, 768, M, x2_c)
+        a_passes(2, (6, 7))
+        add_and_store(2, 4)
+        quantize("x", 3, 768, M, x3_c)
+        a_passes(3, (6, 7))
+        multiply(5, 6)
+        add_and_store(4, 6)
+        multiply(7)
+        add_and_store(6, 7)
+        add_and_store(7, 8)

@@ -57,9 +57,11 @@ def tile_mix_ghost_res_kernel(tc, x, xt, g, gt, r, out):
             load("x", k, 0, 512)
         load("x", 3, 512, 768)
         load("x", 2, 512, M)
-        load_r(0, 4)
+        load_r(0, 2)
+        load_r(2, 4)
         load("x", 3, 768, M)
-        load_r(4, 8)
+        load_r(4, 6)
+        load_r(6, 8)
 
         def interleave(name, k, c0, c1, vector_columns):
             first, tile = [(a, t) for a, b, t in raw[name, k] if a <= c0 and c1 <= b][0]
@@ -149,25 +151,23 @@ def tile_mix_ghost_res_kernel(tc, x, xt, g, gt, r, out):
 
         quantize("x", 3, 0, 512, interleave("x", 3, 0, 512, 320))
         a_passes(3, range(4))
-        x3_b = interleave("x", 3, 512, 768, 96)
-        multiply(0, 1)
+        x3_b = interleave("x", 3, 512, 768, 128)
+        x2_b = interleave("x", 2, 512, 768, 0)
+        x2_c = interleave("x", 2, 768, M, 0)
+        x3_c = interleave("x", 3, 768, M, 0)
+        multiply(0, 1, 2, 3)
         quantize("x", 3, 512, 768, x3_b)
-        x2_b = interleave("x", 2, 512, 768, 64)
-        multiply(2, 3)
+        add_and_store(0, 2)
         quantize("x", 2, 512, 768, x2_b)
         a_passes(2, (4, 5))
         a_passes(3, (4, 5))
-        x2_c = interleave("x", 2, 768, M, 0)
-        x3_c = interleave("x", 3, 768, M, 0)
-        add_and_store(0, 2)
-        multiply(4)
+        add_and_store(2, 4)
+        multiply(4, 5)
         quantize("x", 2, 768, M, x2_c)
         a_passes(2, (6, 7))
-        add_and_store(2, 4)
         quantize("x", 3, 768, M, x3_c)
         a_passes(3, (6, 7))
-        multiply(5, 6)
         add_and_store(4, 6)
-        multiply(7)
+        multiply(6, 7)
         add_and_store(6, 7)
         add_and_store(7, 8)

@@ -55,8 +55,8 @@ def tile_mix_ghost_res_kernel(tc, x, xt, g, gt, r, out):
         for k in (2, 3):
             load("xt", k, 0, N)
             load("x", k, 0, 512)
-        load("x", 3, 512, 768)
         load("x", 2, 512, M)
+        load("x", 3, 512, 768)
         load_r(0, 2)
         load_r(2, 4)
         load("x", 3, 768, M)
@@ -89,7 +89,7 @@ def tile_mix_ghost_res_kernel(tc, x, xt, g, gt, r, out):
 
         def convert(name, k, width):
             pieces = [(c, c + 512) for c in range(0, width, 512)]
-            grouped = [interleave(name, k, c0, c1, 256) for c0, c1 in pieces]
+            grouped = [interleave(name, k, c0, c1, 320) for c0, c1 in pieces]
             for (c0, c1), tile in zip(pieces, grouped):
                 quantize(name, k, c0, c1, tile)
 
@@ -144,27 +144,30 @@ def tile_mix_ghost_res_kernel(tc, x, xt, g, gt, r, out):
         convert("xt", 1, N)
         convert("x", 1, M)
         a_passes(1, range(TILES))
-        convert("xt", 2, N)
-        convert("x", 2, 512)
+        xt2 = interleave("xt", 2, 0, N, 320)
+        x2_a = interleave("x", 2, 0, 512, 320)
+        quantize("xt", 2, 0, N, xt2)
+        xt3 = interleave("xt", 3, 0, N, 320)
+        quantize("x", 2, 0, 512, x2_a)
         a_passes(2, range(4))
-        convert("xt", 3, N)
-
-        quantize("x", 3, 0, 512, interleave("x", 3, 0, 512, 320))
-        a_passes(3, range(4))
-        x3_b = interleave("x", 3, 512, 768, 128)
+        quantize("xt", 3, 0, N, xt3)
+        x3_a = interleave("x", 3, 0, 512, 352)
         x2_b = interleave("x", 2, 512, 768, 0)
-        x2_c = interleave("x", 2, 768, M, 0)
-        x3_c = interleave("x", 3, 768, M, 0)
+        quantize("x", 3, 0, 512, x3_a)
+        a_passes(3, range(4))
         multiply(0, 1, 2, 3)
-        quantize("x", 3, 512, 768, x3_b)
-        add_and_store(0, 2)
         quantize("x", 2, 512, 768, x2_b)
         a_passes(2, (4, 5))
+        x3_b = interleave("x", 3, 512, 768, 0)
+        x2_c = interleave("x", 2, 768, M, 0)
+        x3_c = interleave("x", 3, 768, M, 0)
+        add_and_store(0, 2)
+        quantize("x", 3, 512, 768, x3_b)
         a_passes(3, (4, 5))
         add_and_store(2, 4)
-        multiply(4, 5)
         quantize("x", 2, 768, M, x2_c)
         a_passes(2, (6, 7))
+        multiply(4, 5)
         quantize("x", 3, 768, M, x3_c)
         a_passes(3, (6, 7))
         add_and_store(4, 6)

@@ -17,7 +17,6 @@ ADD = mybir.AluOpType.add
 P = 128
 PACK = 4
 K_PASS = P * PACK
-PASSES = K // K_PASS
 TILES = M // P
 
 
@@ -55,8 +54,8 @@ def tile_mix_ghost_res_kernel(tc, x, xt, g, gt, r, out):
         for k in (2, 3):
             load("xt", k, 0, N)
             load("x", k, 0, 512)
-        load("x", 2, 512, M)
         load("x", 3, 512, 768)
+        load("x", 2, 512, M)
         load_r(0, 2)
         load_r(2, 4)
         load("x", 3, 768, M)
@@ -117,11 +116,11 @@ def tile_mix_ghost_res_kernel(tc, x, xt, g, gt, r, out):
                 u_acc[m] = psum.tile([P, N], F32, name="acc")
                 mx_pass(u_acc[m], "g", "gt", 0, m, True, True)
 
-        def a_passes(k, tiles):
+        def a_passes(k, tiles, last=False):
             for m in tiles:
                 if k == 0:
                     a_acc[m] = psum.tile([P, N], F32, name="acc")
-                mx_pass(a_acc[m], "x", "xt", k, m, k == 0, k == PASSES - 1)
+                mx_pass(a_acc[m], "x", "xt", k, m, k == 0, last)
 
         def multiply(*tiles):
             for m in tiles:
@@ -144,32 +143,35 @@ def tile_mix_ghost_res_kernel(tc, x, xt, g, gt, r, out):
         convert("xt", 1, N)
         convert("x", 1, M)
         a_passes(1, range(TILES))
-        xt2 = interleave("xt", 2, 0, N, 320)
-        x2_a = interleave("x", 2, 0, 512, 320)
+        xt2 = interleave("xt", 2, 0, N, 288)
+        x2_a = interleave("x", 2, 0, 512, 192)
         quantize("xt", 2, 0, N, xt2)
-        xt3 = interleave("xt", 3, 0, N, 320)
+        xt3 = interleave("xt", 3, 0, N, 288)
         quantize("x", 2, 0, 512, x2_a)
         a_passes(2, range(4))
         quantize("xt", 3, 0, N, xt3)
-        x3_a = interleave("x", 3, 0, 512, 352)
-        x2_b = interleave("x", 2, 512, 768, 0)
-        quantize("x", 3, 0, 512, x3_a)
-        a_passes(3, range(4))
+        x3_a = interleave("x", 3, 0, 256, 176)
+        quantize("x", 3, 0, 256, x3_a)
+        a_passes(3, (0, 1), last=True)
+        x3_b = interleave("x", 3, 256, 512, 112)
+        x3_c = interleave("x", 3, 512, 768, 32)
+        x2_c = interleave("x", 2, 512, 768, 0)
+        x2_d = interleave("x", 2, 768, M, 0)
+        x3_d = interleave("x", 3, 768, M, 0)
+        quantize("x", 3, 256, 512, x3_b)
+        a_passes(3, (2, 3), last=True)
         multiply(0, 1, 2, 3)
-        quantize("x", 2, 512, 768, x2_b)
-        a_passes(2, (4, 5))
-        x3_b = interleave("x", 3, 512, 768, 0)
-        x2_c = interleave("x", 2, 768, M, 0)
-        x3_c = interleave("x", 3, 768, M, 0)
-        add_and_store(0, 2)
-        quantize("x", 3, 512, 768, x3_b)
+        quantize("x", 3, 512, 768, x3_c)
         a_passes(3, (4, 5))
+        add_and_store(0, 2)
+        quantize("x", 2, 512, 768, x2_c)
+        a_passes(2, (4, 5), last=True)
         add_and_store(2, 4)
-        quantize("x", 2, 768, M, x2_c)
+        quantize("x", 2, 768, M, x2_d)
         a_passes(2, (6, 7))
         multiply(4, 5)
-        quantize("x", 3, 768, M, x3_c)
-        a_passes(3, (6, 7))
+        quantize("x", 3, 768, M, x3_d)
+        a_passes(3, (6, 7), last=True)
         add_and_store(4, 6)
         multiply(6, 7)
         add_and_store(6, 7)

from contextlib import ExitStack

import concourse.mybir as mybir

K, L, M, N = 2048, 512, 1024, 512
FLOPS = 2 * (K + L) * M * N

F32 = mybir.dt.float32
BF16 = mybir.dt.bfloat16
U32 = mybir.dt.uint32
U8 = mybir.dt.uint8
E4M3 = mybir.dt.float8_e4m3fn_x4
E5M2 = mybir.dt.float8_e5m2_x4
MULT = mybir.AluOpType.mult
ADD = mybir.AluOpType.add

P = 128
PACK = 4
K_PASS = P * PACK
TILES = M // P


def tile_mix_ghost_res_kernel(tc, x, xt, g, gt, r, out):
    nc = tc.nc
    formats = {"x": E4M3, "xt": E4M3, "g": E5M2, "gt": E5M2}
    sources = {"x": x, "xt": xt, "g": g, "gt": gt}

    with ExitStack() as ctx:
        keep = ctx.enter_context(tc.tile_pool(name="keep", bufs=1))
        stage = ctx.enter_context(tc.tile_pool(name="stage", bufs=6))
        psum = ctx.enter_context(tc.psum_pool(name="psum", bufs=8))
        ctx.enter_context(tc.manual_schedule())

        raw = {}
        r_rows = {}

        def load(name, k, c0, c1):
            tile = keep.tile([P, PACK, c1 - c0], F32, name="raw_%s_%d_%d" % (name, k, c0))
            rows = sources[name][k * K_PASS : (k + 1) * K_PASS, c0:c1]
            nc.sync.dma_start(out=tile[:], in_=rows.rearrange("(p j) w -> p j w", j=PACK))
            raw[name, k] = raw.get((name, k), []) + [(c0, c1, tile)]

        def load_r(t0, t1):
            tile = keep.tile([P, t1 - t0, N], F32, name="r_%d" % t0)
            nc.sync.dma_start(out=tile[:], in_=r[t0 * P : t1 * P, :].rearrange("(t p) n -> p t n", p=P))
            for t in range(t0, t1):
                r_rows[t] = (t0, tile)

        load("gt", 0, 0, N)
        load("g", 0, 0, M)
        for k in (0, 1):
            load("xt", k, 0, N)
            load("x", k, 0, M)
        for k in (2, 3):
            load("xt", k, 0, N)
            load("x", k, 0, 512)
        load("x", 3, 512, 768)
        load("x", 2, 512, M)
        load_r(0, 2)
        load_r(2, 4)
        load("x", 3, 768, M)
        load_r(4, 6)
        load_r(6, 8)

        def interleave(name, k, c0, c1, vector_columns):
            first, tile = [(a, t) for a, b, t in raw[name, k] if a <= c0 and c1 <= b][0]
            grouped = stage.tile([P, c1 - c0, PACK], BF16, name="grouped", align_bytes=64)
            for engine_copy, lo, hi in (
                (nc.scalar.copy, vector_columns, c1 - c0),
                (nc.vector.tensor_copy, 0, vector_columns),
            ):
                if lo < hi:
                    engine_copy(
                        out=grouped[:, lo:hi, :].rearrange("p (c i) j -> p c j i", i=4),
                        in_=tile[:, :, c0 - first + lo : c0 - first + hi].rearrange("p j (c i) -> p c j i", i=4),
                    )
            return grouped

        quantized = {}

        def quantize(name, k, c0, c1, grouped):
            codes = keep.tile([P, c1 - c0], U32, name="codes_%s_%d_%d" % (name, k, c0), align_bytes=64)
            scales = keep.tile([P, c1 - c0], U8, name="scales_%s_%d_%d" % (name, k, c0), align_bytes=64)
            nc.vector.quantize_mx(
                out=codes[:].bitcast(formats[name]), scales=scales[:], in_=grouped[:].rearrange("p w j -> p (w j)")
            )
            quantized[name, k] = quantized.get((name, k), []) + [(c0, c1, codes, scales)]

        def convert(name, k, width):
            pieces = [(c, c + 512) for c in range(0, width, 512)]
            grouped = [interleave(name, k, c0, c1, 320) for c0, c1 in pieces]
            for (c0, c1), tile in zip(pieces, grouped):
                quantize(name, k, c0, c1, tile)

        def mx_pass(acc, left, right, k, m, start, stop):
            c0, codes, scales = [(a, co, sc) for a, b, co, sc in quantized[left, k] if a <= m * P < b][0]
            cols = slice(m * P - c0, (m + 1) * P - c0)
            right_codes, right_scales = quantized[right, k][0][2:]
            nc.tensor.matmul_mx(
                out=acc[:],
                lhsT=codes[:, cols].bitcast(formats[left]),
                lhsT_scale=scales[:, cols],
                rhs=right_codes[:].bitcast(formats[right]),
                rhs_scale=right_scales[:],
                start=start,
                stop=stop,
            )

        u_acc = {}
        u = keep.tile([P, TILES, N], F32, name="u")
        a_acc = {}
        result = keep.tile([P, TILES, N], F32, name="result")

        def u_passes():
            for m in range(TILES):
                u_acc[m] = psum.tile([P, N], F32, name="acc")
                mx_pass(u_acc[m], "g", "gt", 0, m, True, True)

        def a_passes(k, tiles, last=False):
            for m in tiles:
                if k == 0:
                    a_acc[m] = psum.tile([P, N], F32, name="acc")
                mx_pass(a_acc[m], "x", "xt", k, m, k == 0, last)

        def multiply(*tiles):
            for m in tiles:
                nc.vector.tensor_tensor(out=result[:, m, :], in0=a_acc[m][:], in1=u[:, m, :], op=MULT)

        def add_and_store(t0, t1):
            first, tile = r_rows[t0]
            sums = result[:, t0:t1, :]
            nc.vector.tensor_tensor(out=sums, in0=sums, in1=tile[:, t0 - first : t1 - first, :], op=ADD)
            nc.sync.dma_start(out=out[t0 * P : t1 * P, :].rearrange("(t p) n -> p t n", p=P), in_=sums)

        convert("gt", 0, N)
        convert("g", 0, M)
        u_passes()
        convert("xt", 0, N)
        for m in range(TILES):
            nc.scalar.copy(out=u[:, m, :], in_=u_acc[m][:])
        convert("x", 0, M)
        a_passes(0, range(TILES))
        convert("xt", 1, N)
        convert("x", 1, M)
        a_passes(1, range(TILES))
        xt2 = interleave("xt", 2, 0, N, 288)
        x2_a = interleave("x", 2, 0, 512, 192)
        quantize("xt", 2, 0, N, xt2)
        xt3 = interleave("xt", 3, 0, N, 288)
        quantize("x", 2, 0, 512, x2_a)
        a_passes(2, range(4))
        quantize("xt", 3, 0, N, xt3)
        x3_a = interleave("x", 3, 0, 256, 176)
        quantize("x", 3, 0, 256, x3_a)
        a_passes(3, (0, 1), last=True)
        x3_b = interleave("x", 3, 256, 512, 112)
        x3_c = interleave("x", 3, 512, 768, 32)
        x2_c = interleave("x", 2, 512, 768, 0)
        x2_d = interleave("x", 2, 768, M, 0)
        x3_d = interleave("x", 3, 768, M, 0)
        quantize("x", 3, 256, 512, x3_b)
        a_passes(3, (2, 3), last=True)
        multiply(0, 1, 2, 3)
        quantize("x", 3, 512, 768, x3_c)
        a_passes(3, (4, 5))
        add_and_store(0, 2)
        quantize("x", 2, 512, 768, x2_c)
        a_passes(2, (4, 5), last=True)
        add_and_store(2, 4)
        quantize("x", 2, 768, M, x2_d)
        a_passes(2, (6, 7))
        multiply(4, 5)
        quantize("x", 3, 768, M, x3_d)
        a_passes(3, (6, 7), last=True)
        add_and_store(4, 6)
        multiply(6, 7)
        add_and_store(6, 7)
        add_and_store(7, 8)
